import numpy as np
import ml_dtypes


def mxq(x, axis, fmt="e4m3"):
    dtype, down = {"e4m3": (ml_dtypes.float8_e4m3fn, 7), "e5m2": (ml_dtypes.float8_e5m2, 14)}[fmt]
    v = np.moveaxis(np.asarray(x, np.float32).astype(ml_dtypes.bfloat16).astype(np.float64), axis, -1)
    blocks = v.reshape(v.shape[:-1] + (-1, 32))
    amax = np.abs(blocks).max(-1, keepdims=True)
    byte = np.maximum(np.where(amax > 0, np.frexp(amax)[1] - 1 + 127, 0) - down, 1)
    scale = np.exp2(byte - 127.0)
    codes = (blocks / scale).astype(np.float32).astype(dtype).astype(np.float64)
    return np.moveaxis((codes * scale).reshape(v.shape), -1, axis)


WIDE = False


def mx_kscale(k):
    if not WIDE:
        return np.ones(k)
    levels = np.array([30, -30])
    if k % 512:
        return np.exp2(np.random.permutation(np.resize(levels, k // 32))).repeat(32)
    a = np.empty((k // 512, 16))
    for p in range(k // 512):
        a[p, :8] = np.random.permutation(np.resize(levels, 8))
        for g in range(8):
            far = levels[np.abs(levels - a[p, g]) >= 10]
            a[p, g + 8] = far[np.random.randint(len(far))]
    return np.exp2(a.ravel()).repeat(32)


def f64(x):
    return np.asarray(x).astype(np.float64)


def striped(idx):
    return np.tile(np.asarray(idx).reshape(-1, 16).T, (8, 1)).astype(np.uint16)


def unstriped(offs):
    return offs[:16].T.reshape(-1).astype(np.int64)


E2M1 = np.array([0.0, 0.5, 1.0, 1.5, 2.0, 3.0, 4.0, 6.0, -0.0, -0.5, -1.0, -1.5, -2.0, -3.0, -4.0, -6.0])


def pack_weight(w, fmt):
    k, n = w.shape
    w = f64(np.asarray(w, np.float32).astype(ml_dtypes.bfloat16)).reshape(k // 32, 32, n)
    amax = np.abs(w).max(1)
    if fmt in ("e4m3", "e5m2"):
        byte = np.frexp(amax)[1] - 1 + 127 - (7 if fmt == "e4m3" else 14)
    else:
        mant, ex = np.frexp(amax / 6.0)
        byte = np.where(mant > 0.5, ex, ex - 1) + 127
    byte = np.clip(np.where(amax > 0, byte, 1), 1, 254)
    scaled = (w * np.exp2(127.0 - byte)[:, None, :]).reshape(k, n).astype(np.float32)
    by_word = np.ascontiguousarray(scaled.reshape(k // 512, 128, 4, n).transpose(0, 1, 3, 2))
    if fmt in ("e4m3", "e5m2"):
        words = by_word.astype(ml_dtypes.float8_e4m3fn if fmt == "e4m3" else ml_dtypes.float8_e5m2).view(np.uint8)
    else:
        c = by_word.astype(ml_dtypes.float4_e2m1fn).view(np.uint8) & 0xF
        words = (c[..., 0::2] | (c[..., 1::2] << 4)).reshape(k // 512, 128, 2 * n)
    return np.ascontiguousarray(words), np.ascontiguousarray(byte.astype(np.uint8).reshape(k // 512, 16, n))


def unpack_weight(words, scales, fmt):
    g, _, n = scales.shape
    words = np.ascontiguousarray(words).reshape(g, 128, n, -1)
    if fmt in ("e4m3", "e5m2"):
        vals = words.view(ml_dtypes.float8_e4m3fn if fmt == "e4m3" else ml_dtypes.float8_e5m2).astype(np.float64)
    else:
        nib = np.empty((g, 128, n, 4), np.uint8)
        nib[..., 0::2] = words & 0xF
        nib[..., 1::2] = words >> 4
        vals = E2M1[nib]
    vals = vals * np.repeat(np.exp2(scales.astype(np.float64) - 127.0), 8, axis=1)[..., None]
    return vals.transpose(0, 1, 3, 2).reshape(g * 512, n)


K, F, T, Z, J, R, O, N, E = 512, 512, 1024, 1024, 256, 512, 128, 256, 1024


def setup_inputs():
    n = np.random.standard_normal
    idx = np.random.permutation(T)[:J]
    idx2 = np.random.permutation(Z)[:J]
    idx3 = np.random.permutation(J)[:O]
    idx4 = np.random.permutation(T)[:O]
    idx5 = np.random.permutation(E)[:O]
    fk = mx_kscale(K)
    fr = mx_kscale(R)
    ff = mx_kscale(F)
    xtp = pack_weight(n((K, T)) / fk[:, None], "e4m3")
    wp = pack_weight(n((K, R)) * 1 / np.sqrt(K) * fk[:, None] * fr, "e2m1")
    xop = pack_weight(n((F, Z)) / ff[:, None], "e2m1")
    w0p = pack_weight(n((F, R)) * 1 / np.sqrt(F) * ff[:, None] * fr, "e5m2")
    wbp = pack_weight(n((R, N)) * 1 / np.sqrt(R) / fr[:, None], "e5m2")
    wsp = pack_weight(n((K, N)) * 1 / np.sqrt(K) * fk[:, None], "e5m2")
    return {
        "xt_words": xtp[0],
        "xt_scales": xtp[1],
        "w_words": wp[0],
        "w_scales": wp[1],
        "xo_words": xop[0],
        "xo_scales": xop[1],
        "w0_words": w0p[0],
        "w0_scales": w0p[1],
        "sa": (np.random.uniform(0.5, 1.6, (R, 1))).astype(np.float32),
        "wb_words": wbp[0],
        "wb_scales": wbp[1],
        "ws_words": wsp[0],
        "ws_scales": wsp[1],
        "offs": striped(idx),
        "offs2": striped(idx2),
        "offs3": striped(idx3),
        "offs4": striped(idx4),
        "offs5": striped(idx5),
    }


def reference(xt_words, xt_scales, w_words, w_scales, xo_words, xo_scales, w0_words, w0_scales, sa, wb_words, wb_scales, ws_words, ws_scales, offs, offs2, offs3, offs4, offs5):
    idx = unstriped(offs)
    idx2 = unstriped(offs2)
    idx3 = unstriped(offs3)
    idx4 = unstriped(offs4)
    idx5 = unstriped(offs5)
    xtu = unpack_weight(xt_words, xt_scales, "e4m3")
    wu = unpack_weight(w_words, w_scales, "e2m1")
    xou = unpack_weight(xo_words, xo_scales, "e2m1")
    w0u = unpack_weight(w0_words, w0_scales, "e5m2")
    wbu = unpack_weight(wb_words, wb_scales, "e5m2")
    wsu = unpack_weight(ws_words, ws_scales, "e5m2")
    xtidxg = xtu[:, idx]
    xoidx2g = xou[:, idx2]
    a = wu.T @ xtidxg + w0u.T @ xoidx2g
    g1 = np.maximum(a, 0.0)
    hid = g1[:, idx3] * f64(sa)
    hidq = mxq(hid, 0, "e4m3")
    xtidx4g = xtu[:, idx4]
    p = wbu.T @ hidq + wsu.T @ xtidx4g
    y = np.zeros((N, E))
    y[:, idx5] = p
    return y

from contextlib import ExitStack

import concourse.mybir as mybir

F32 = mybir.dt.float32
BF16 = mybir.dt.bfloat16
I32 = mybir.dt.int32
U32 = mybir.dt.uint32
U16 = mybir.dt.uint16
U8 = mybir.dt.uint8
E4M3 = mybir.dt.float8_e4m3fn_x4
E5M2 = mybir.dt.float8_e5m2_x4
E2M1 = mybir.dt.float4_e2m1fn_x4
COPY = mybir.ActivationFunctionType.Copy

P = 128
PACK = 4
T, Z, J, R, O, N, E = 1024, 1024, 256, 512, 128, 256, 1024
K = F = 512
FLOPS = 2 * (K * R * J + F * R * J + R * N * O + K * N * O)


def tile_list_keptpositive_bank_further_scattered_kernel(
    tc, xt_words, xt_scales, w_words, w_scales, xo_words, xo_scales, w0_words, w0_scales, sa,
    wb_words, wb_scales, ws_words, ws_scales, offs, offs2, offs3, offs4, offs5, out,
):
    nc = tc.nc
    with ExitStack() as ctx:
        lists = ctx.enter_context(tc.tile_pool(name="lists", bufs=1))
        sb = ctx.enter_context(tc.tile_pool(name="sb", bufs=1))
        psum = ctx.enter_context(tc.psum_pool(name="psum", bufs=1))

        def tile(name, cols, dtype):
            return sb.tile([P, cols], dtype, name=name, align_bytes=64)

        def load_list(name, src):
            t = lists.tile(list(src.shape), U16, name=name)
            nc.sync.dma_start(t[:], src)
            return t

        def load_words8(queue, name, src):
            t = tile(name, src.shape[2], I32)
            queue.dma_start(t[:], src[0].rearrange("p n t -> p (n t)").bitcast(I32))
            return t

        def load_words4(queue, name, src):
            t = tile(name, src.shape[2] // 2, U16)
            queue.dma_start(t[:].bitcast(I32), src[0].bitcast(I32))
            return t

        def zero_plane(name, cols):
            t = tile(name, cols, U8)
            nc.vector.memset(t[:].bitcast(I32), 0)
            return t

        def load_plane(queue, t, src, quads):
            for q in quads:
                queue.dma_start(t[32 * q : 32 * q + 4, :].bitcast(I32), src[0, 4 * q : 4 * q + 4, :].bitcast(I32))

        xt_s = zero_plane("xt_s", T)
        raw_s = sb.tile([P, 2 * R], U8, name="raw_s", tag="page0", align_bytes=64)
        nc.vector.memset(raw_s[:].bitcast(I32), 0)
        xo_s = zero_plane("xo_s", Z)
        ws_s = zero_plane("ws_s", N)
        wb_s = zero_plane("wb_s", N)
        stage = sb.tile([4, 4, 2 * R], U8, name="stage", tag="page1", align_bytes=64)

        idx = load_list("idx", offs)
        for i, src in enumerate((w_scales, w0_scales)):
            nc.scalar.dma_start(
                stage[:, :, i * R : (i + 1) * R].bitcast(I32), src[0].rearrange("(q r) n -> r q n", r=4).bitcast(I32)
            )
        load_plane(nc.sync, xt_s, xt_scales, range(2))
        load_plane(nc.scalar, xt_s, xt_scales, range(2, 4))
        xt_w = load_words8(nc.sync, "xt_w", xt_words)
        w_w = load_words4(nc.gpsimd, "w_w", w_words)
        w0_w = load_words8(nc.gpsimd, "w0_w", w0_words)
        idx2 = load_list("idx2", offs2)
        load_plane(nc.sync, xo_s, xo_scales, range(4))
        xo_w = load_words4(nc.sync, "xo_w", xo_words)
        idx3 = load_list("idx3", offs3)
        sa_t = tile("sa_t", PACK, F32)
        nc.sync.dma_start(sa_t[:], sa.rearrange("(p t) o -> p (t o)", t=PACK))
        idx4 = load_list("idx4", offs4)
        load_plane(nc.sync, ws_s, ws_scales, range(4))
        ws_w = load_words8(nc.sync, "ws_w", ws_words)
        wb_w = load_words8(nc.sync, "wb_w", wb_words)
        load_plane(nc.sync, wb_s, wb_scales, range(4))
        idx5 = load_list("idx5", offs5)

        for q in range(4):
            nc.vector.tensor_copy(raw_s[32 * q : 32 * q + 4, :].bitcast(I32), stage[:, q, :].bitcast(I32))

        def gather(name, window, offsets, cols, dtype):
            t = tile(name, cols, dtype)
            nc.vector.tensor_copy(t[:], window.indirect(offsets[:]))
            return t

        def deal(copy, name, src, dtype, run):
            t = tile(name, R, dtype)
            copy(
                out=t[:].rearrange("p (t a b) -> p a t b", t=PACK, b=run),
                in_=src.rearrange("p (a b t) -> p a t b", t=PACK, b=run),
            )
            return t

        xt_gs = gather("xt_gs", xt_s[:], idx, J, U8)
        xt_gw = gather("xt_gw", xt_w[:].bitcast(U32), idx, J, U32)
        w_ds = deal(nc.gpsimd.tensor_copy, "w_ds", raw_s[:, 0:R], U8, 16)
        w0_ds = deal(nc.gpsimd.tensor_copy, "w0_ds", raw_s[:, R : 2 * R], U8, 16)
        w_d = deal(nc.scalar.copy, "w_d", w_w[:], U16, 8)
        xo_gs = gather("xo_gs", xo_s[:], idx2, J, U8)
        xo_gw = gather("xo_gw", xo_w[:], idx2, J, U16)
        w0_d = []
        for t in range(PACK):
            piece = tile("w0_d%d" % t, P, U32)
            nc.scalar.copy(piece[:], w0_w[:].bitcast(U32).rearrange("p (m t) -> p t m", t=PACK)[:, t, :])
            w0_d.append(piece)

        pages = [sb.tile([P, E], F32, name="page%d" % h, tag="page%d" % h, align_bytes=64) for h in range(N // P)]
        for page in pages:
            nc.gpsimd.memset(page[:], 0.0)

        acc = [psum.tile([P, J], F32, name="acc%d" % t) for t in range(PACK)]
        for t in range(PACK):
            cols = slice(t * P, (t + 1) * P)
            nc.tensor.matmul_mx(
                acc[t][:], lhsT=w_d[:, cols].bitcast(E2M1), lhsT_scale=w_ds[:, cols],
                rhs=xt_gw[:].bitcast(E4M3), rhs_scale=xt_gs[:], start=True, stop=False,
            )
        hid = sb.tile([P, PACK, O], BF16, name="hid", align_bytes=64)
        for t in range(PACK):
            cols = slice(t * P, (t + 1) * P)
            nc.tensor.matmul_mx(
                acc[t][:], lhsT=w0_d[t][:].bitcast(E5M2), lhsT_scale=w0_ds[:, cols],
                rhs=xo_gw[:].bitcast(E2M1), rhs_scale=xo_gs[:], start=False, stop=True,
            )
            g1 = tile("g1_%d" % t, J, F32)
            nc.vector.tensor_scalar_max(g1[:], acc[t][:], 0.0)
            nc.scalar.activation(hid[:, t, :], g1[:].indirect(idx3[:]), COPY, scale=sa_t[:, t : t + 1])

        xt4_gw = gather("xt4_gw", xt_w[:].bitcast(U32), idx4, O, U32)
        xt4_gs = gather("xt4_gs", xt_s[:], idx4, O, U8)
        res = [psum.tile([P, O], F32, name="res%d" % h) for h in range(N // P)]
        for h in range(N // P):
            cols = slice(h * P, (h + 1) * P)
            nc.tensor.matmul_mx(
                res[h][:], lhsT=ws_w[:, cols].bitcast(E5M2), lhsT_scale=ws_s[:, cols],
                rhs=xt4_gw[:].bitcast(E4M3), rhs_scale=xt4_gs[:], start=True, stop=False,
            )

        woven = sb.tile([P, O, PACK], BF16, name="woven", align_bytes=64)
        nc.vector.tensor_copy(
            woven[:].rearrange("p (c i) t -> p c t i", i=4), hid[:].rearrange("p t (c i) -> p c t i", i=4)
        )
        hid_w = tile("hid_w", O, U32)
        hid_s = tile("hid_s", O, U8)
        nc.vector.quantize_mx(hid_w[:].bitcast(E4M3), hid_s[:], woven[:].rearrange("p o t -> p (o t)"))

        for h in range(N // P):
            cols = slice(h * P, (h + 1) * P)
            nc.tensor.matmul_mx(
                res[h][:], lhsT=wb_w[:, cols].bitcast(E5M2), lhsT_scale=wb_s[:, cols],
                rhs=hid_w[:].bitcast(E4M3), rhs_scale=hid_s[:], start=False, stop=True,
            )
        vals = [tile("val%d" % h, O, F32) for h in range(N // P)]
        nc.vector.tensor_copy(vals[0][:], res[0][:])
        nc.vector.tensor_copy(pages[0][:].indirect(idx5[:]), vals[0][:])
        nc.sync.dma_start(out[0:P, :], pages[0][:])
        nc.scalar.copy(vals[1][:], res[1][:])
        nc.scalar.activation(pages[1][:].indirect(idx5[:]), vals[1][:], COPY)
        nc.scalar.dma_start(out[P : 2 * P, :], pages[1][:])
